import numpy as np
import ml_dtypes


def mxq(x, axis, fmt="e4m3"):
    dtype, down = {"e4m3": (ml_dtypes.float8_e4m3fn, 7), "e5m2": (ml_dtypes.float8_e5m2, 14)}[fmt]
    v = np.moveaxis(np.asarray(x, np.float32).astype(ml_dtypes.bfloat16).astype(np.float64), axis, -1)
    blocks = v.reshape(v.shape[:-1] + (-1, 32))
    amax = np.abs(blocks).max(-1, keepdims=True)
    byte = np.maximum(np.where(amax > 0, np.frexp(amax)[1] - 1 + 127, 0) - down, 1)
    scale = np.exp2(byte - 127.0)
    codes = (blocks / scale).astype(np.float32).astype(dtype).astype(np.float64)
    return np.moveaxis((codes * scale).reshape(v.shape), -1, axis)


WIDE = False


def mx_kscale(k):
    if not WIDE:
        return np.ones(k)
    levels = np.array([10, -10, 5, -5, 0])
    if k % 512:
        return np.exp2(np.random.permutation(np.resize(levels, k // 32))).repeat(32)
    a = np.empty((k // 512, 16))
    for p in range(k // 512):
        a[p, :8] = np.random.permutation(np.resize(levels, 8))
        for g in range(8):
            far = levels[np.abs(levels - a[p, g]) >= 10]
            a[p, g + 8] = far[np.random.randint(len(far))]
    return np.exp2(a.ravel()).repeat(32)


def f64(x):
    return np.asarray(x).astype(np.float64)


def striped(idx):
    return np.tile(idx.reshape(-1, 16).T, (8, 1)).astype(np.uint16)


def unstriped(offs):
    return offs[:16].T.reshape(-1).astype(np.int64)


K, T, E, C, N = 512, 1280, 6, 128, 512


def by_expert(wq, xq):
    return np.concatenate([wq[e].T @ xq[:, e * C:(e + 1) * C] for e in range(E)], axis=1)


def setup_inputs():
    n = np.random.standard_normal
    s = mx_kscale(N)[:, None]
    return {
        "dyT": (n((N, T)) * s).astype(np.float32),
        "w": (n((E + 1, N, K)) / np.sqrt(N) / s[None]).astype(np.float32),
        "gate": np.tile(np.random.uniform(0.2, 1.0, E * C), (N, 1)).astype(np.float32),
        "offs": striped(np.random.permutation(T)[:E * C]),
    }


def reference(dyT, w, gate, offs):
    idx = unstriped(offs)
    gq = mxq(f64(gate) * f64(dyT)[:, idx], 0, "e4m3")
    wq = mxq(f64(w), 1, "e4m3")
    ds = wq[E].T @ mxq(f64(dyT), 0, "e4m3")
    dx = by_expert(wq, gq)
    ds[:, idx] += dx
    return ds

@@ -1,0 +1,176 @@
+from contextlib import ExitStack
+
+import concourse.mybir as mybir
+
+K, T, E, C, N = 512, 1280, 6, 128, 512
+S = E * C
+FLOPS = 2 * N * K * (S + T)
+BYTES = 4 * (N * T + (E + 1) * N * K + 128 * S + K * T) + 2 * 128 * (S // 16)
+
+F32 = mybir.dt.float32
+BF16 = mybir.dt.bfloat16
+U32 = mybir.dt.uint32
+U16 = mybir.dt.uint16
+U8 = mybir.dt.uint8
+FP8X4 = mybir.dt.float8_e4m3fn_x4
+MULT = mybir.AluOpType.mult
+ADD = mybir.AluOpType.add
+
+P = 128
+PACK = 4
+PIECE = 256
+PIECES = S // PIECE
+BLOCKS = K // P
+BANK = 512
+HALF = 256
+CHUNKS = [(0, 512), (512, 1024), (1024, 1280)]
+
+
+def tile_moe_bds_lin_none_kernel(tc, dyT, w, gate, offs, out):
+    nc = tc.nc
+    with ExitStack() as ctx:
+        keep = ctx.enter_context(tc.tile_pool(name="keep", bufs=1))
+        dx_psum = ctx.enter_context(tc.psum_pool(name="dx_psum", bufs=2))
+        ds_psum = ctx.enter_context(tc.psum_pool(name="ds_psum", bufs=6))
+
+        offsets = keep.tile([P, S // 16], U16, name="offsets")
+        nc.sync.dma_start(offsets[:], offs)
+        dy = keep.tile([P, PACK, T], F32, name="dy", align_bytes=64)
+        dy_rows = dyT.rearrange("(p t) c -> p t c", t=PACK)
+        for t in range(PACK):
+            nc.sync.dma_start(dy[:, t, :], dy_rows[:, t, :])
+        gates = keep.tile([P, S], F32, name="gates", align_bytes=64)
+        nc.sync.dma_start(gates[:], gate[0:P, :])
+        w_raw = []
+        for e in range(E + 1):
+            raw = keep.tile([P, PACK, K], F32, name="w_raw%d" % e, align_bytes=64)
+            nc.sync.dma_start(raw[:], w[e].rearrange("(p t) k -> p t k", t=PACK))
+            w_raw.append(raw)
+
+        routed = []
+        for m in range(BLOCKS):
+            z = keep.tile([P, T], F32, name="routed%d" % m, align_bytes=64)
+            (nc.vector if m < 2 else nc.gpsimd).memset(z[:].bitcast(U32), 0)
+            routed.append(z)
+
+        def interleave(name, src, lo, hi):
+            dst = keep.tile([P, (hi - lo) * PACK], BF16, name=name, align_bytes=64)
+            nc.scalar.copy(
+                dst[:].rearrange("p (c i t) -> p c t i", i=4, t=PACK),
+                src[:, :, lo:hi].rearrange("p t (c i) -> p c t i", i=4),
+            )
+            return dst
+
+        def quantize(name, src):
+            width = src.shape[1] // PACK
+            codes = keep.tile([P, width], U32, name=name + "_codes", align_bytes=64)
+            scales = keep.tile([P, width], U8, name=name + "_scales", align_bytes=64)
+            nc.vector.quantize_mx(out=codes[:].bitcast(FP8X4), scales=scales[:], in_=src[:])
+            return codes, scales
+
+        def product(acc, stationary, s_cols, moving, m_cols):
+            nc.tensor.matmul_mx(
+                out=acc,
+                lhsT=stationary[0][:, s_cols].bitcast(FP8X4),
+                lhsT_scale=stationary[1][:, s_cols],
+                rhs=moving[0][:, m_cols].bitcast(FP8X4),
+                rhs_scale=moving[1][:, m_cols],
+                start=True,
+                stop=True,
+            )
+
+        def offsets_of(j):
+            return offsets[:, j * PIECE // 16 : (j + 1) * PIECE // 16]
+
+        picked = keep.tile([P, PACK, S], F32, name="picked", align_bytes=64)
+        for t in range(PACK):
+            nc.vector.tensor_copy(picked[:, t, :], dy[:, t, :].indirect(offsets[:]))
+
+        dy_bf = {}
+        dy_q = {}
+        w_bf = {}
+        w_q = {}
+        g_bf = {}
+        g_q = {}
+
+        def cast_w(e):
+            for h in range(2):
+                w_bf[e, h] = interleave("w_bf%d_%d" % (e, h), w_raw[e], h * HALF, (h + 1) * HALF)
+
+        def quant_w(e):
+            for h in range(2):
+                w_q[e, h] = quantize("w%d_%d" % (e, h), w_bf[e, h])
+
+        dy_bf[0] = interleave("dy_bf0", dy, *CHUNKS[0])
+        cast_w(0)
+        cast_w(1)
+        for j in range(PIECES):
+            cols = slice(j * PIECE, (j + 1) * PIECE)
+            g = keep.tile([P, PIECE * PACK], BF16, name="g_bf%d" % j, align_bytes=64)
+            nc.vector.tensor_tensor(
+                g[:].rearrange("p (c i t) -> p c t i", i=2, t=PACK),
+                picked[:, :, cols].rearrange("p t (c i) -> p c t i", i=2),
+                gates[:, cols].rearrange("p (c o i) -> p c o i", o=1, i=2).to_broadcast([P, PIECE // 2, PACK, 2]),
+                MULT,
+            )
+            g_bf[j] = g
+        for j in range(PIECES):
+            g_q[j] = quantize("g%d" % j, g_bf[j])
+        dy_q[0] = quantize("dy0", dy_bf[0])
+
+        dx_sb = {}
+
+        def routed_products(j):
+            for h in range(2):
+                acc = dx_psum.tile([P, BANK], F32, name="dx_acc")
+                for mm in range(2):
+                    for ee in range(2):
+                        col = mm * PIECE + ee * C
+                        product(acc[:, col : col + C], w_q[2 * j + ee, h], slice(mm * P, (mm + 1) * P),
+                                g_q[j], slice(ee * C, (ee + 1) * C))
+                sb = keep.tile([P, BANK], F32, name="dx%d_%d" % (j, h), align_bytes=64)
+                nc.scalar.copy(sb[:], acc[:])
+                dx_sb[j, h] = sb
+
+        def scatter(j, m):
+            src = dx_sb[j, m // 2][:, (m % 2) * PIECE : (m % 2 + 1) * PIECE]
+            nc.vector.tensor_copy(routed[m][:].indirect(offsets_of(j)), src)
+
+        def finish(m):
+            for i, (lo, hi) in enumerate(CHUNKS):
+                acc = ds_psum.tile([P, BANK], F32, name="ds_acc")
+                product(acc[:, 0 : hi - lo], w_q[E, m // 2], slice((m % 2) * P, (m % 2 + 1) * P), dy_q[i], slice(0, hi - lo))
+                res = keep.tile([P, hi - lo], F32, name="res%d_%d" % (m, i), align_bytes=64)
+                nc.vector.tensor_tensor(res[:], acc[:, 0 : hi - lo], routed[m][:, lo:hi], ADD)
+                nc.sync.dma_start(out[m * P : (m + 1) * P, lo:hi], res[:])
+
+        quant_w(0)
+        quant_w(1)
+        routed_products(0)
+        cast_w(2)
+        cast_w(3)
+        for m in range(BLOCKS):
+            scatter(0, m)
+        quant_w(2)
+        quant_w(3)
+        routed_products(1)
+        for i in (1, 2):
+            dy_bf[i] = interleave("dy_bf%d" % i, dy, *CHUNKS[i])
+        cast_w(4)
+        cast_w(5)
+        scatter(1, 0)
+        scatter(1, 1)
+        for i in (1, 2):
+            dy_q[i] = quantize("dy%d" % i, dy_bf[i])
+        scatter(1, 2)
+        quant_w(4)
+        quant_w(5)
+        routed_products(2)
+        cast_w(E)
+        scatter(1, 3)
+        quant_w(E)
+        scatter(2, 0)
+        for m in range(1, BLOCKS):
+            scatter(2, m)
+            finish(m - 1)
+        finish(BLOCKS - 1)

@@ -23,6 +23,7 @@ PIECES = S // PIECE
 BLOCKS = K // P
 BANK = 512
 HALF = 256
+GP_BLOCKS = (0, 1, 2)
 CHUNKS = [(0, 512), (512, 1024), (1024, 1280)]
 
 
@@ -30,8 +31,8 @@ def tile_moe_bds_lin_none_kernel(tc, dyT, w, gate, offs, out):
     nc = tc.nc
     with ExitStack() as ctx:
         keep = ctx.enter_context(tc.tile_pool(name="keep", bufs=1))
-        dx_psum = ctx.enter_context(tc.psum_pool(name="dx_psum", bufs=2))
-        ds_psum = ctx.enter_context(tc.psum_pool(name="ds_psum", bufs=6))
+        dx_psum = ctx.enter_context(tc.psum_pool(name="dx_psum", bufs=3))
+        ds_psum = ctx.enter_context(tc.psum_pool(name="ds_psum", bufs=5))
 
         offsets = keep.tile([P, S // 16], U16, name="offsets")
         nc.sync.dma_start(offsets[:], offs)
@@ -86,25 +87,26 @@ def tile_moe_bds_lin_none_kernel(tc, dyT, w, gate, offs, out):
         for t in range(PACK):
             nc.vector.tensor_copy(picked[:, t, :], dy[:, t, :].indirect(offsets[:]))
 
-        dy_bf = {}
+        dy_bf = [keep.tile([P, (hi - lo) * PACK], BF16, name="dy_bf%d" % i, align_bytes=64) for i, (lo, hi) in enumerate(CHUNKS)]
         dy_q = {}
-        w_bf = {}
         w_q = {}
-        g_bf = {}
         g_q = {}
+        dx_acc = {}
 
-        def cast_w(e):
-            for h in range(2):
-                w_bf[e, h] = interleave("w_bf%d_%d" % (e, h), w_raw[e], h * HALF, (h + 1) * HALF)
+        def cast_dy(c):
+            i, part = divmod(c, 2)
+            nc.scalar.copy(
+                dy_bf[i][:, part * HALF * PACK : (part + 1) * HALF * PACK].rearrange("p (c i t) -> p c t i", i=4, t=PACK),
+                dy[:, :, c * HALF : (c + 1) * HALF].rearrange("p t (c i) -> p c t i", i=4),
+            )
 
-        def quant_w(e):
-            for h in range(2):
-                w_q[e, h] = quantize("w%d_%d" % (e, h), w_bf[e, h])
+        def quant_dy(i):
+            dy_q[i] = quantize("dy%d" % i, dy_bf[i])
 
-        dy_bf[0] = interleave("dy_bf0", dy, *CHUNKS[0])
-        cast_w(0)
-        cast_w(1)
-        for j in range(PIECES):
+        def weights(e, h):
+            w_q[e, h] = quantize("w%d_%d" % (e, h), interleave("w_bf%d_%d" % (e, h), w_raw[e], h * HALF, (h + 1) * HALF))
+
+        def gated(j):
             cols = slice(j * PIECE, (j + 1) * PIECE)
             g = keep.tile([P, PIECE * PACK], BF16, name="g_bf%d" % j, align_bytes=64)
             nc.vector.tensor_tensor(
@@ -113,64 +115,80 @@ def tile_moe_bds_lin_none_kernel(tc, dyT, w, gate, offs, out):
                 gates[:, cols].rearrange("p (c o i) -> p c o i", o=1, i=2).to_broadcast([P, PIECE // 2, PACK, 2]),
                 MULT,
             )
-            g_bf[j] = g
-        for j in range(PIECES):
-            g_q[j] = quantize("g%d" % j, g_bf[j])
-        dy_q[0] = quantize("dy0", dy_bf[0])
+            return g
 
-        dx_sb = {}
+        def routed_products(j, h):
+            acc = dx_psum.tile([P, BANK], F32, name="dx_acc")
+            for mm in range(2):
+                for ee in range(2):
+                    col = mm * PIECE + ee * C
+                    product(acc[:, col : col + C], w_q[2 * j + ee, h], slice(mm * P, (mm + 1) * P),
+                            g_q[j], slice(ee * C, (ee + 1) * C))
+            dx_acc[j, h] = acc
 
-        def routed_products(j):
-            for h in range(2):
-                acc = dx_psum.tile([P, BANK], F32, name="dx_acc")
-                for mm in range(2):
-                    for ee in range(2):
-                        col = mm * PIECE + ee * C
-                        product(acc[:, col : col + C], w_q[2 * j + ee, h], slice(mm * P, (mm + 1) * P),
-                                g_q[j], slice(ee * C, (ee + 1) * C))
-                sb = keep.tile([P, BANK], F32, name="dx%d_%d" % (j, h), align_bytes=64)
-                nc.scalar.copy(sb[:], acc[:])
-                dx_sb[j, h] = sb
-
-        def scatter(j, m):
-            src = dx_sb[j, m // 2][:, (m % 2) * PIECE : (m % 2 + 1) * PIECE]
-            nc.vector.tensor_copy(routed[m][:].indirect(offsets_of(j)), src)
+        def put_back(j, m):
+            sb = keep.tile([P, PIECE], F32, name="dx%d_%d" % (j, m), align_bytes=64)
+            nc.scalar.copy(sb[:], dx_acc[j, m // 2][:, (m % 2) * PIECE : (m % 2 + 1) * PIECE])
+            nc.vector.tensor_copy(routed[m][:].indirect(offsets_of(j)), sb[:])
 
         def finish(m):
             for i, (lo, hi) in enumerate(CHUNKS):
                 acc = ds_psum.tile([P, BANK], F32, name="ds_acc")
                 product(acc[:, 0 : hi - lo], w_q[E, m // 2], slice((m % 2) * P, (m % 2 + 1) * P), dy_q[i], slice(0, hi - lo))
                 res = keep.tile([P, hi - lo], F32, name="res%d_%d" % (m, i), align_bytes=64)
-                nc.vector.tensor_tensor(res[:], acc[:, 0 : hi - lo], routed[m][:, lo:hi], ADD)
+                if m in GP_BLOCKS:
+                    nc.scalar.copy(res[:], acc[:, 0 : hi - lo])
+                    nc.gpsimd.tensor_tensor(res[:], res[:], routed[m][:, lo:hi], ADD)
+                else:
+                    nc.vector.tensor_tensor(res[:], acc[:, 0 : hi - lo], routed[m][:, lo:hi], ADD)
                 nc.sync.dma_start(out[m * P : (m + 1) * P, lo:hi], res[:])
 
-        quant_w(0)
-        quant_w(1)
-        routed_products(0)
-        cast_w(2)
-        cast_w(3)
-        for m in range(BLOCKS):
-            scatter(0, m)
-        quant_w(2)
-        quant_w(3)
-        routed_products(1)
-        for i in (1, 2):
-            dy_bf[i] = interleave("dy_bf%d" % i, dy, *CHUNKS[i])
-        cast_w(4)
-        cast_w(5)
-        scatter(1, 0)
-        scatter(1, 1)
-        for i in (1, 2):
-            dy_q[i] = quantize("dy%d" % i, dy_bf[i])
-        scatter(1, 2)
-        quant_w(4)
-        quant_w(5)
-        routed_products(2)
-        cast_w(E)
-        scatter(1, 3)
-        quant_w(E)
-        scatter(2, 0)
-        for m in range(1, BLOCKS):
-            scatter(2, m)
-            finish(m - 1)
-        finish(BLOCKS - 1)
+        for c in range(3):
+            cast_dy(c)
+        g0 = gated(0)
+        g1 = gated(1)
+        g_q[0] = quantize("g0", g0)
+        g2 = gated(2)
+        weights(0, 0)
+        weights(1, 0)
+        routed_products(0, 0)
+        g_q[1] = quantize("g1", g1)
+        g_q[2] = quantize("g2", g2)
+        quant_dy(0)
+        weights(0, 1)
+        weights(1, 1)
+        routed_products(0, 1)
+        put_back(0, 0)
+        put_back(0, 1)
+        weights(2, 0)
+        weights(3, 0)
+        routed_products(1, 0)
+        put_back(0, 2)
+        weights(2, 1)
+        put_back(0, 3)
+        weights(4, 0)
+        put_back(1, 0)
+        weights(5, 0)
+        routed_products(2, 0)
+        put_back(1, 1)
+        weights(3, 1)
+        routed_products(1, 1)
+        cast_dy(3)
+        quant_dy(1)
+        weights(E, 0)
+        put_back(2, 0)
+        cast_dy(4)
+        quant_dy(2)
+        put_back(2, 1)
+        weights(4, 1)
+        weights(5, 1)
+        routed_products(2, 1)
+        put_back(1, 2)
+        finish(0)
+        weights(E, 1)
+        put_back(2, 2)
+        finish(1)
+        put_back(1, 3)
+        put_back(2, 3)
+        finish(2)
+        finish(3)

@@ -18,13 +18,11 @@ ADD = mybir.AluOpType.add
 
 P = 128
 PACK = 4
-PIECE = 256
-PIECES = S // PIECE
+COLS = 256
+UNIT = COLS * PACK
 BLOCKS = K // P
 BANK = 512
-HALF = 256
-GP_BLOCKS = (0, 1, 2)
-CHUNKS = [(0, 512), (512, 1024), (1024, 1280)]
+SHARED = E
 
 
 def tile_moe_bds_lin_none_kernel(tc, dyT, w, gate, offs, out):
@@ -34,161 +32,219 @@ def tile_moe_bds_lin_none_kernel(tc, dyT, w, gate, offs, out):
         dx_psum = ctx.enter_context(tc.psum_pool(name="dx_psum", bufs=3))
         ds_psum = ctx.enter_context(tc.psum_pool(name="ds_psum", bufs=5))
 
+        def sbuf(name, shape, dtype, tag=""):
+            return keep.tile(shape, dtype, name=name, tag=tag, align_bytes=64)
+
         offsets = keep.tile([P, S // 16], U16, name="offsets")
         nc.sync.dma_start(offsets[:], offs)
-        dy = keep.tile([P, PACK, T], F32, name="dy", align_bytes=64)
+        dy = sbuf("dy", [P, PACK, T], F32)
         dy_rows = dyT.rearrange("(p t) c -> p t c", t=PACK)
         for t in range(PACK):
             nc.sync.dma_start(dy[:, t, :], dy_rows[:, t, :])
-        gates = keep.tile([P, S], F32, name="gates", align_bytes=64)
-        nc.sync.dma_start(gates[:], gate[0:P, :])
-        w_raw = []
+
+        w_raw = {}
+
+        def load_w(e, h):
+            w_raw[e, h] = sbuf("w_raw%d_%d" % (e, h), [P, PACK, COLS], F32)
+            rows = w[e].rearrange("(p t) k -> p t k", t=PACK)
+            nc.sync.dma_start(w_raw[e, h][:], rows[:, :, h * COLS : (h + 1) * COLS])
+
+        gates_first = sbuf("gates_first", [P, 2 * COLS], F32)
+        nc.sync.dma_start(gates_first[:], gate[0:P, 0 : 2 * COLS])
+        load_w(0, 0)
+        load_w(1, 0)
+        gates_last = sbuf("gates_last", [P, COLS], F32)
+        nc.sync.dma_start(gates_last[:], gate[0:P, 2 * COLS : S])
+        for e in range(2, E + 1):
+            load_w(e, 0)
         for e in range(E + 1):
-            raw = keep.tile([P, PACK, K], F32, name="w_raw%d" % e, align_bytes=64)
-            nc.sync.dma_start(raw[:], w[e].rearrange("(p t) k -> p t k", t=PACK))
-            w_raw.append(raw)
+            load_w(e, 1)
+        gates = [gates_first[:, 0:COLS], gates_first[:, COLS : 2 * COLS], gates_last[:]]
 
         routed = []
         for m in range(BLOCKS):
-            z = keep.tile([P, T], F32, name="routed%d" % m, align_bytes=64)
-            (nc.vector if m < 2 else nc.gpsimd).memset(z[:].bitcast(U32), 0)
-            routed.append(z)
+            window = sbuf("routed%d" % m, [P, T], F32)
+            (nc.vector if m < 2 else nc.gpsimd).memset(window[:].bitcast(U32), 0)
+            routed.append(window)
 
-        def interleave(name, src, lo, hi):
-            dst = keep.tile([P, (hi - lo) * PACK], BF16, name=name, align_bytes=64)
+        picked = sbuf("picked", [P, PACK, S], F32)
+        for t in range(PACK):
+            nc.vector.tensor_copy(picked[:, t, :], dy[:, t, :].indirect(offsets[:]))
+
+        def piece(ap, i):
+            return ap[:, :, i * COLS : (i + 1) * COLS]
+
+        def unit_of(tile, i):
+            return tile[:, i * UNIT : (i + 1) * UNIT]
+
+        def round_on_scalar(dst, src):
             nc.scalar.copy(
-                dst[:].rearrange("p (c i t) -> p c t i", i=4, t=PACK),
-                src[:, :, lo:hi].rearrange("p t (c i) -> p c t i", i=4),
+                dst.rearrange("p (c i t) -> p c t i", i=4, t=PACK),
+                src.rearrange("p t (c i) -> p c t i", i=4),
             )
-            return dst
 
-        def quantize(name, src):
-            width = src.shape[1] // PACK
-            codes = keep.tile([P, width], U32, name=name + "_codes", align_bytes=64)
-            scales = keep.tile([P, width], U8, name=name + "_scales", align_bytes=64)
-            nc.vector.quantize_mx(out=codes[:].bitcast(FP8X4), scales=scales[:], in_=src[:])
-            return codes, scales
+        def round_on_gpsimd(dst, src):
+            nc.gpsimd.tensor_scalar(
+                dst.rearrange("p (c t) -> p c t", t=PACK), src.rearrange("p t c -> p c t"), 1.0, 0.0, MULT, ADD
+            )
 
-        def product(acc, stationary, s_cols, moving, m_cols):
+        def gate_and_round(dst, j):
+            nc.vector.tensor_tensor(
+                dst.rearrange("p (c i t) -> p c t i", i=2, t=PACK),
+                piece(picked, j).rearrange("p t (c i) -> p c t i", i=2),
+                gates[j].rearrange("p (c o i) -> p c o i", o=1, i=2).to_broadcast([P, COLS // 2, PACK, 2]),
+                MULT,
+            )
+
+        mx = {}
+
+        def quantize(src, keys, tag=""):
+            width = COLS * len(keys)
+            name = "_".join(str(part) for key in keys for part in key)
+            codes = sbuf("codes_" + name, [P, width], U32, tag)
+            scales = sbuf("scales_" + name, [P, width], U8)
+            nc.vector.quantize_mx(out=codes[:].bitcast(FP8X4), scales=scales[:], in_=src)
+            for i, key in enumerate(keys):
+                mx[key] = (codes, scales, i * COLS)
+
+        def product(acc, w_key, m, moving_key, lo, width):
+            w_codes, w_scales, w_at = mx[w_key]
+            codes, scales, at = mx[moving_key]
+            w_cols = slice(w_at + (m % 2) * P, w_at + (m % 2 + 1) * P)
+            cols = slice(at + lo, at + lo + width)
             nc.tensor.matmul_mx(
                 out=acc,
-                lhsT=stationary[0][:, s_cols].bitcast(FP8X4),
-                lhsT_scale=stationary[1][:, s_cols],
-                rhs=moving[0][:, m_cols].bitcast(FP8X4),
-                rhs_scale=moving[1][:, m_cols],
+                lhsT=w_codes[:, w_cols].bitcast(FP8X4),
+                lhsT_scale=w_scales[:, w_cols],
+                rhs=codes[:, cols].bitcast(FP8X4),
+                rhs_scale=scales[:, cols],
                 start=True,
                 stop=True,
             )
 
-        def offsets_of(j):
-            return offsets[:, j * PIECE // 16 : (j + 1) * PIECE // 16]
-
-        picked = keep.tile([P, PACK, S], F32, name="picked", align_bytes=64)
-        for t in range(PACK):
-            nc.vector.tensor_copy(picked[:, t, :], dy[:, t, :].indirect(offsets[:]))
-
-        dy_bf = [keep.tile([P, (hi - lo) * PACK], BF16, name="dy_bf%d" % i, align_bytes=64) for i, (lo, hi) in enumerate(CHUNKS)]
-        dy_q = {}
-        w_q = {}
-        g_q = {}
-        dx_acc = {}
-
-        def cast_dy(c):
-            i, part = divmod(c, 2)
-            nc.scalar.copy(
-                dy_bf[i][:, part * HALF * PACK : (part + 1) * HALF * PACK].rearrange("p (c i t) -> p c t i", i=4, t=PACK),
-                dy[:, :, c * HALF : (c + 1) * HALF].rearrange("p t (c i) -> p c t i", i=4),
-            )
-
-        def quant_dy(i):
-            dy_q[i] = quantize("dy%d" % i, dy_bf[i])
-
-        def weights(e, h):
-            w_q[e, h] = quantize("w%d_%d" % (e, h), interleave("w_bf%d_%d" % (e, h), w_raw[e], h * HALF, (h + 1) * HALF))
-
-        def gated(j):
-            cols = slice(j * PIECE, (j + 1) * PIECE)
-            g = keep.tile([P, PIECE * PACK], BF16, name="g_bf%d" % j, align_bytes=64)
-            nc.vector.tensor_tensor(
-                g[:].rearrange("p (c i t) -> p c t i", i=2, t=PACK),
-                picked[:, :, cols].rearrange("p t (c i) -> p c t i", i=2),
-                gates[:, cols].rearrange("p (c o i) -> p c o i", o=1, i=2).to_broadcast([P, PIECE // 2, PACK, 2]),
-                MULT,
-            )
-            return g
+        dx_banks = {}
 
         def routed_products(j, h):
-            acc = dx_psum.tile([P, BANK], F32, name="dx_acc")
-            for mm in range(2):
-                for ee in range(2):
-                    col = mm * PIECE + ee * C
-                    product(acc[:, col : col + C], w_q[2 * j + ee, h], slice(mm * P, (mm + 1) * P),
-                            g_q[j], slice(ee * C, (ee + 1) * C))
-            dx_acc[j, h] = acc
+            bank = dx_psum.tile([P, BANK], F32, name="dx_bank")
+            for m in range(2):
+                for e in range(2):
+                    at = m * COLS + e * C
+                    product(bank[:, at : at + C], ("w", 2 * j + e, h), m, ("g", j), e * C, C)
+            dx_banks[j, h] = bank
 
-        def put_back(j, m):
-            sb = keep.tile([P, PIECE], F32, name="dx%d_%d" % (j, m), align_bytes=64)
-            nc.scalar.copy(sb[:], dx_acc[j, m // 2][:, (m % 2) * PIECE : (m % 2 + 1) * PIECE])
-            nc.vector.tensor_copy(routed[m][:].indirect(offsets_of(j)), sb[:])
+        def put_back(j, m, spent):
+            nc.scalar.copy(spent, dx_banks[j, m // 2][:, (m % 2) * COLS : (m % 2 + 1) * COLS])
+            entries = offsets[:, j * COLS // 16 : (j + 1) * COLS // 16]
+            nc.vector.tensor_copy(routed[m][:].indirect(entries), spent)
 
-        def finish(m):
-            for i, (lo, hi) in enumerate(CHUNKS):
-                acc = ds_psum.tile([P, BANK], F32, name="ds_acc")
-                product(acc[:, 0 : hi - lo], w_q[E, m // 2], slice((m % 2) * P, (m % 2 + 1) * P), dy_q[i], slice(0, hi - lo))
-                res = keep.tile([P, hi - lo], F32, name="res%d_%d" % (m, i), align_bytes=64)
-                if m in GP_BLOCKS:
-                    nc.scalar.copy(res[:], acc[:, 0 : hi - lo])
-                    nc.gpsimd.tensor_tensor(res[:], res[:], routed[m][:, lo:hi], ADD)
-                else:
-                    nc.vector.tensor_tensor(res[:], acc[:, 0 : hi - lo], routed[m][:, lo:hi], ADD)
-                nc.sync.dma_start(out[m * P : (m + 1) * P, lo:hi], res[:])
+        def shared_product(m, lo):
+            hi = min(lo + BANK, T)
+            bank = ds_psum.tile([P, BANK], F32, name="ds_bank")
+            for at in range(lo, hi, COLS):
+                product(bank[:, at - lo : at - lo + COLS], ("w", SHARED, m // 2), m, ("dy", at // COLS), 0, COLS)
+            return bank[:, 0 : hi - lo]
 
-        for c in range(3):
-            cast_dy(c)
-        g0 = gated(0)
-        g1 = gated(1)
-        g_q[0] = quantize("g0", g0)
-        g2 = gated(2)
-        weights(0, 0)
-        weights(1, 0)
+        ds = {m: sbuf("ds%d" % m, [P, T], F32) for m in range(BLOCKS - 1)}
+
+        def shared_to_sbuf(m, *starts):
+            for lo in starts:
+                nc.scalar.copy(ds[m][:, lo : min(lo + BANK, T)], shared_product(m, lo))
+
+        def add_on_gpsimd(m, half, tag=""):
+            cols = slice(half * T // 2, (half + 1) * T // 2)
+            total = sbuf("total%d_%d" % (m, half), [P, T // 2], F32, tag)
+            nc.gpsimd.tensor_tensor(total[:], ds[m][:, cols], routed[m][:, cols], ADD)
+            nc.sync.dma_start(out[m * P : (m + 1) * P, cols], total[:])
+
+        def add_on_vector(m):
+            for lo in range(0, T, BANK):
+                hi = min(lo + BANK, T)
+                total = sbuf("total%d_%d" % (m, lo), [P, hi - lo], F32)
+                nc.vector.tensor_tensor(total[:], shared_product(m, lo), routed[m][:, lo:hi], ADD)
+                nc.sync.dma_start(out[m * P : (m + 1) * P, lo:hi], total[:])
+
+        def weights(experts, h):
+            tag = "w_bf%d_%d" % (experts[0], h)
+            staged = sbuf(tag, [P, len(experts) * UNIT], BF16, tag)
+            for i, e in enumerate(experts):
+                round_on_scalar(unit_of(staged, i), w_raw[e, h][:])
+            quantize(staged[:], [("w", e, h) for e in experts])
+            return tag
+
+        dy_first = sbuf("dy_first", [P, 2 * UNIT], BF16)
+        for c in range(2):
+            round_on_scalar(unit_of(dy_first, c), piece(dy, c))
+        g_bf = sbuf("g_bf", [P, 3 * UNIT], BF16)
+        gate_and_round(unit_of(g_bf, 0), 0)
+        gate_and_round(unit_of(g_bf, 1), 1)
+        quantize(unit_of(g_bf, 0), [("g", 0)])
+        spent_tag = weights([0], 0)
+        quantize(unit_of(g_bf, 1), [("g", 1)], spent_tag)
+        spent_tag = weights([1], 0)
         routed_products(0, 0)
-        g_q[1] = quantize("g1", g1)
-        g_q[2] = quantize("g2", g2)
-        quant_dy(0)
-        weights(0, 1)
-        weights(1, 1)
-        routed_products(0, 1)
-        put_back(0, 0)
-        put_back(0, 1)
-        weights(2, 0)
-        weights(3, 0)
+        quantize(dy_first[:], [("dy", 0), ("dy", 1)], spent_tag)
+        gate_and_round(unit_of(g_bf, 2), 2)
+        quantize(unit_of(g_bf, 2), [("g", 2)])
+
+        duo = sbuf("duo", [P, 2 * UNIT], BF16)
+        trio = sbuf("trio", [P, 3 * UNIT], BF16)
+        round_on_scalar(unit_of(duo, 0), w_raw[2, 0][:])
+        quantize(unit_of(duo, 0), [("w", 2, 0)])
+        round_on_gpsimd(unit_of(duo, 0), piece(dy, 2))
+        put_back(0, 0, w_raw[2, 0][:, 0, :])
+
+        round_on_scalar(unit_of(trio, 1), w_raw[3, 0][:])
+        quantize(unit_of(trio, 1), [("w", 3, 0)])
         routed_products(1, 0)
-        put_back(0, 2)
-        weights(2, 1)
-        put_back(0, 3)
-        weights(4, 0)
-        put_back(1, 0)
-        weights(5, 0)
+        round_on_gpsimd(unit_of(trio, 1), piece(dy, 3))
+        put_back(0, 1, w_raw[3, 0][:, 0, :])
+
+        round_on_scalar(unit_of(duo, 1), w_raw[4, 0][:])
+        quantize(duo[:], [("dy", 2), ("w", 4, 0)])
+        round_on_scalar(unit_of(trio, 2), w_raw[5, 0][:])
+        quantize(trio[:, UNIT : 3 * UNIT], [("dy", 3), ("w", 5, 0)])
         routed_products(2, 0)
-        put_back(1, 1)
-        weights(3, 1)
+        round_on_gpsimd(unit_of(trio, 1), piece(dy, 4))
+        put_back(1, 0, w_raw[5, 0][:, 0, :])
+
+        round_on_scalar(unit_of(trio, 0), w_raw[SHARED, 0][:])
+        quantize(trio[:, 0 : 2 * UNIT], [("w", SHARED, 0), ("dy", 4)])
+
+        def rounded(e, staged, i):
+            round_on_scalar(unit_of(staged, i), w_raw[e, 1][:])
+            return w_raw[e, 1]
+
+        pairs = [sbuf("pair%d" % j, [P, 2 * UNIT], BF16, "pair%d" % j) for j in range(3)]
+        put_back(1, 1, rounded(0, pairs[0], 0)[:, 0, :])
+        rounded(1, pairs[0], 1)
+        quantize(pairs[0][:], [("w", 0, 1), ("w", 1, 1)])
+        routed_products(0, 1)
+        put_back(2, 0, rounded(2, pairs[1], 0)[:, 0, :])
+        spent = rounded(3, pairs[1], 1)
+        quantize(pairs[1][:], [("w", 2, 1), ("w", 3, 1)])
         routed_products(1, 1)
-        cast_dy(3)
-        quant_dy(1)
-        weights(E, 0)
-        put_back(2, 0)
-        cast_dy(4)
-        quant_dy(2)
-        put_back(2, 1)
-        weights(4, 1)
-        weights(5, 1)
+        put_back(2, 1, spent[:, 0, :])
+        shared_to_sbuf(0, 0, BANK)
+        rounded(4, pairs[2], 0)
+        spent = rounded(5, pairs[2], 1)
+        quantize(pairs[2][:], [("w", 4, 1), ("w", 5, 1)])
         routed_products(2, 1)
-        put_back(1, 2)
-        finish(0)
-        weights(E, 1)
-        put_back(2, 2)
-        finish(1)
-        put_back(1, 3)
-        put_back(2, 3)
-        finish(2)
-        finish(3)
+        add_on_gpsimd(0, 0, "pair2")
+        put_back(0, 2, spent[:, 0, :])
+        spent_tag = weights([SHARED], 1)
+        last = w_raw[SHARED, 1]
+        put_back(0, 3, last[:, 0, :])
+        shared_to_sbuf(0, 2 * BANK)
+        add_on_gpsimd(0, 1, spent_tag)
+        put_back(1, 2, last[:, 1, :])
+        shared_to_sbuf(1, 0, BANK, 2 * BANK)
+        add_on_gpsimd(1, 0)
+        add_on_gpsimd(1, 1)
+        put_back(2, 2, last[:, 2, :])
+        shared_to_sbuf(2, 0, BANK)
+        put_back(1, 3, last[:, 3, :])
+        shared_to_sbuf(2, 2 * BANK)
+        put_back(2, 3, spent[:, 1, :])
+        add_on_gpsimd(2, 0)
+        add_on_gpsimd(2, 1)
+        add_on_vector(3)

@@ -23,6 +23,7 @@ UNIT = COLS * PACK
 BLOCKS = K // P
 BANK = 512
 SHARED = E
+PER_COLUMN = 16
 
 
 def tile_moe_bds_lin_none_kernel(tc, dyT, w, gate, offs, out):
@@ -35,7 +36,7 @@ def tile_moe_bds_lin_none_kernel(tc, dyT, w, gate, offs, out):
         def sbuf(name, shape, dtype, tag=""):
             return keep.tile(shape, dtype, name=name, tag=tag, align_bytes=64)
 
-        offsets = keep.tile([P, S // 16], U16, name="offsets")
+        offsets = keep.tile([P, S // PER_COLUMN], U16, name="offsets")
         nc.sync.dma_start(offsets[:], offs)
         dy = sbuf("dy", [P, PACK, T], F32)
         dy_rows = dyT.rearrange("(p t) c -> p t c", t=PACK)
@@ -64,15 +65,15 @@ def tile_moe_bds_lin_none_kernel(tc, dyT, w, gate, offs, out):
         routed = []
         for m in range(BLOCKS):
             window = sbuf("routed%d" % m, [P, T], F32)
-            (nc.vector if m < 2 else nc.gpsimd).memset(window[:].bitcast(U32), 0)
+            nc.gpsimd.memset(window[:].bitcast(U32), 0)
             routed.append(window)
 
         picked = sbuf("picked", [P, PACK, S], F32)
         for t in range(PACK):
             nc.vector.tensor_copy(picked[:, t, :], dy[:, t, :].indirect(offsets[:]))
 
-        def piece(ap, i):
-            return ap[:, :, i * COLS : (i + 1) * COLS]
+        def dy_piece(c):
+            return dy[:, :, c * COLS : (c + 1) * COLS]
 
         def unit_of(tile, i):
             return tile[:, i * UNIT : (i + 1) * UNIT]
@@ -91,7 +92,7 @@ def tile_moe_bds_lin_none_kernel(tc, dyT, w, gate, offs, out):
         def gate_and_round(dst, j):
             nc.vector.tensor_tensor(
                 dst.rearrange("p (c i t) -> p c t i", i=2, t=PACK),
-                piece(picked, j).rearrange("p t (c i) -> p c t i", i=2),
+                picked[:, :, j * COLS : (j + 1) * COLS].rearrange("p t (c i) -> p c t i", i=2),
                 gates[j].rearrange("p (c o i) -> p c o i", o=1, i=2).to_broadcast([P, COLS // 2, PACK, 2]),
                 MULT,
             )
@@ -101,22 +102,22 @@ def tile_moe_bds_lin_none_kernel(tc, dyT, w, gate, offs, out):
         def quantize(src, keys, tag=""):
             width = COLS * len(keys)
             name = "_".join(str(part) for key in keys for part in key)
-            codes = sbuf("codes_" + name, [P, width], U32, tag)
+            words = sbuf("words_" + name, [P, width], U32, tag)
             scales = sbuf("scales_" + name, [P, width], U8)
-            nc.vector.quantize_mx(out=codes[:].bitcast(FP8X4), scales=scales[:], in_=src)
+            nc.vector.quantize_mx(out=words[:].bitcast(FP8X4), scales=scales[:], in_=src)
             for i, key in enumerate(keys):
-                mx[key] = (codes, scales, i * COLS)
+                mx[key] = (words, scales, i * COLS)
 
-        def product(acc, w_key, m, moving_key, lo, width):
-            w_codes, w_scales, w_at = mx[w_key]
-            codes, scales, at = mx[moving_key]
+        def product(acc, e, m, moving_key, lo, width):
+            w_words, w_scales, w_at = mx["w", e, m // 2]
+            words, scales, at = mx[moving_key]
             w_cols = slice(w_at + (m % 2) * P, w_at + (m % 2 + 1) * P)
             cols = slice(at + lo, at + lo + width)
             nc.tensor.matmul_mx(
                 out=acc,
-                lhsT=w_codes[:, w_cols].bitcast(FP8X4),
+                lhsT=w_words[:, w_cols].bitcast(FP8X4),
                 lhsT_scale=w_scales[:, w_cols],
-                rhs=codes[:, cols].bitcast(FP8X4),
+                rhs=words[:, cols].bitcast(FP8X4),
                 rhs_scale=scales[:, cols],
                 start=True,
                 stop=True,
@@ -126,125 +127,115 @@ def tile_moe_bds_lin_none_kernel(tc, dyT, w, gate, offs, out):
 
         def routed_products(j, h):
             bank = dx_psum.tile([P, BANK], F32, name="dx_bank")
-            for m in range(2):
+            for i in range(2):
                 for e in range(2):
-                    at = m * COLS + e * C
-                    product(bank[:, at : at + C], ("w", 2 * j + e, h), m, ("g", j), e * C, C)
+                    at = i * COLS + e * C
+                    product(bank[:, at : at + C], 2 * j + e, 2 * h + i, ("g", j), e * C, C)
             dx_banks[j, h] = bank
 
         def put_back(j, m, spent):
             nc.scalar.copy(spent, dx_banks[j, m // 2][:, (m % 2) * COLS : (m % 2 + 1) * COLS])
-            entries = offsets[:, j * COLS // 16 : (j + 1) * COLS // 16]
+            entries = offsets[:, j * COLS // PER_COLUMN : (j + 1) * COLS // PER_COLUMN]
             nc.vector.tensor_copy(routed[m][:].indirect(entries), spent)
 
         def shared_product(m, lo):
             hi = min(lo + BANK, T)
             bank = ds_psum.tile([P, BANK], F32, name="ds_bank")
             for at in range(lo, hi, COLS):
-                product(bank[:, at - lo : at - lo + COLS], ("w", SHARED, m // 2), m, ("dy", at // COLS), 0, COLS)
+                product(bank[:, at - lo : at - lo + COLS], SHARED, m, ("dy", at // COLS), 0, COLS)
             return bank[:, 0 : hi - lo]
 
-        ds = {m: sbuf("ds%d" % m, [P, T], F32) for m in range(BLOCKS - 1)}
+        ds = [sbuf("ds%d" % m, [P, T], F32) for m in range(BLOCKS)]
 
         def shared_to_sbuf(m, *starts):
             for lo in starts:
                 nc.scalar.copy(ds[m][:, lo : min(lo + BANK, T)], shared_product(m, lo))
 
-        def add_on_gpsimd(m, half, tag=""):
-            cols = slice(half * T // 2, (half + 1) * T // 2)
-            total = sbuf("total%d_%d" % (m, half), [P, T // 2], F32, tag)
-            nc.gpsimd.tensor_tensor(total[:], ds[m][:, cols], routed[m][:, cols], ADD)
-            nc.sync.dma_start(out[m * P : (m + 1) * P, cols], total[:])
+        def add_on_gpsimd(m, lo, hi, tag=""):
+            total = sbuf("total%d_%d" % (m, lo), [P, hi - lo], F32, tag)
+            nc.gpsimd.tensor_tensor(total[:], ds[m][:, lo:hi], routed[m][:, lo:hi], ADD)
+            nc.sync.dma_start(out[m * P : (m + 1) * P, lo:hi], total[:])
 
-        def add_on_vector(m):
-            for lo in range(0, T, BANK):
-                hi = min(lo + BANK, T)
-                total = sbuf("total%d_%d" % (m, lo), [P, hi - lo], F32)
-                nc.vector.tensor_tensor(total[:], shared_product(m, lo), routed[m][:, lo:hi], ADD)
-                nc.sync.dma_start(out[m * P : (m + 1) * P, lo:hi], total[:])
+        def add_on_vector(m, lo):
+            total = sbuf("total%d_%d" % (m, lo), [P, BANK], F32)
+            nc.vector.tensor_tensor(total[:], shared_product(m, lo), routed[m][:, lo : lo + BANK], ADD)
+            nc.sync.dma_start(out[m * P : (m + 1) * P, lo : lo + BANK], total[:])
 
-        def weights(experts, h):
-            tag = "w_bf%d_%d" % (experts[0], h)
-            staged = sbuf(tag, [P, len(experts) * UNIT], BF16, tag)
-            for i, e in enumerate(experts):
-                round_on_scalar(unit_of(staged, i), w_raw[e, h][:])
-            quantize(staged[:], [("w", e, h) for e in experts])
+        def lone_half(e, h):
+            tag = "w_bf%d_%d" % (e, h)
+            staged = sbuf(tag, [P, UNIT], BF16, tag)
+            round_on_scalar(staged[:], w_raw[e, h][:])
+            quantize(staged[:], [("w", e, h)])
             return tag
 
-        dy_first = sbuf("dy_first", [P, 2 * UNIT], BF16)
-        for c in range(2):
-            round_on_scalar(unit_of(dy_first, c), piece(dy, c))
-        g_bf = sbuf("g_bf", [P, 3 * UNIT], BF16)
-        gate_and_round(unit_of(g_bf, 0), 0)
-        gate_and_round(unit_of(g_bf, 1), 1)
-        quantize(unit_of(g_bf, 0), [("g", 0)])
-        spent_tag = weights([0], 0)
-        quantize(unit_of(g_bf, 1), [("g", 1)], spent_tag)
-        spent_tag = weights([1], 0)
+        early = sbuf("early", [P, 4 * UNIT], BF16)
+        g_first = sbuf("g_first", [P, 2 * UNIT], BF16)
+        for i in range(2):
+            round_on_scalar(unit_of(early, i), dy_piece(i))
+        round_on_gpsimd(unit_of(early, 2), dy_piece(2))
+        for j in range(2):
+            gate_and_round(unit_of(g_first, j), j)
+        quantize(unit_of(g_first, 0), [("g", 0)])
+        quantize(unit_of(g_first, 1), [("g", 1)], lone_half(0, 0))
+        spent_unit = lone_half(1, 0)
         routed_products(0, 0)
-        quantize(dy_first[:], [("dy", 0), ("dy", 1)], spent_tag)
-        gate_and_round(unit_of(g_bf, 2), 2)
-        quantize(unit_of(g_bf, 2), [("g", 2)])
+        gate_and_round(unit_of(early, 3), 2)
+        quantize(early[:], [("dy", 0), ("dy", 1), ("dy", 2), ("g", 2)], spent_unit)
 
-        duo = sbuf("duo", [P, 2 * UNIT], BF16)
-        trio = sbuf("trio", [P, 3 * UNIT], BF16)
-        round_on_scalar(unit_of(duo, 0), w_raw[2, 0][:])
-        quantize(unit_of(duo, 0), [("w", 2, 0)])
-        round_on_gpsimd(unit_of(duo, 0), piece(dy, 2))
-        put_back(0, 0, w_raw[2, 0][:, 0, :])
+        strip = sbuf("strip", [P, 8 * UNIT], BF16)
 
-        round_on_scalar(unit_of(trio, 1), w_raw[3, 0][:])
-        quantize(unit_of(trio, 1), [("w", 3, 0)])
+        def fill(first_unit, halves):
+            for i, (e, h) in enumerate(halves):
+                round_on_scalar(unit_of(strip, first_unit + i), w_raw[e, h][:])
+            return [("w", e, h) for e, h in halves]
+
+        quantize(strip[:, 0 : 2 * UNIT], fill(0, [(2, 0), (3, 0)]))
         routed_products(1, 0)
-        round_on_gpsimd(unit_of(trio, 1), piece(dy, 3))
-        put_back(0, 1, w_raw[3, 0][:, 0, :])
+        round_on_gpsimd(unit_of(strip, 1), dy_piece(3))
+        put_back(0, 0, w_raw[3, 0][:, 0, :])
+        put_back(0, 1, w_raw[3, 0][:, 1, :])
 
-        round_on_scalar(unit_of(duo, 1), w_raw[4, 0][:])
-        quantize(duo[:], [("dy", 2), ("w", 4, 0)])
-        round_on_scalar(unit_of(trio, 2), w_raw[5, 0][:])
-        quantize(trio[:, UNIT : 3 * UNIT], [("dy", 3), ("w", 5, 0)])
+        quantize(strip[:, UNIT : 5 * UNIT], [("dy", 3)] + fill(2, [(4, 0), (5, 0), (SHARED, 0)]))
         routed_products(2, 0)
-        round_on_gpsimd(unit_of(trio, 1), piece(dy, 4))
-        put_back(1, 0, w_raw[5, 0][:, 0, :])
+        round_on_gpsimd(unit_of(strip, 4), dy_piece(4))
+        put_back(1, 0, w_raw[SHARED, 0][:, 0, :])
+        put_back(1, 1, w_raw[SHARED, 0][:, 1, :])
 
-        round_on_scalar(unit_of(trio, 0), w_raw[SHARED, 0][:])
-        quantize(trio[:, 0 : 2 * UNIT], [("w", SHARED, 0), ("dy", 4)])
-
-        def rounded(e, staged, i):
-            round_on_scalar(unit_of(staged, i), w_raw[e, 1][:])
-            return w_raw[e, 1]
-
-        pairs = [sbuf("pair%d" % j, [P, 2 * UNIT], BF16, "pair%d" % j) for j in range(3)]
-        put_back(1, 1, rounded(0, pairs[0], 0)[:, 0, :])
-        rounded(1, pairs[0], 1)
-        quantize(pairs[0][:], [("w", 0, 1), ("w", 1, 1)])
+        quantize(strip[:, 4 * UNIT : 8 * UNIT], [("dy", 4)] + fill(5, [(0, 1), (1, 1), (2, 1)]))
         routed_products(0, 1)
-        put_back(2, 0, rounded(2, pairs[1], 0)[:, 0, :])
-        spent = rounded(3, pairs[1], 1)
-        quantize(pairs[1][:], [("w", 2, 1), ("w", 3, 1)])
+        put_back(2, 0, w_raw[2, 1][:, 0, :])
+
+        pairs = [sbuf("pair%d" % i, [P, 2 * UNIT], BF16, "pair%d" % i) for i in range(2)]
+        for i in range(2):
+            round_on_scalar(unit_of(pairs[0], i), w_raw[3 + i, 1][:])
+        quantize(pairs[0][:], [("w", 3, 1), ("w", 4, 1)])
         routed_products(1, 1)
-        put_back(2, 1, spent[:, 0, :])
+        put_back(2, 1, w_raw[4, 1][:, 0, :])
         shared_to_sbuf(0, 0, BANK)
-        rounded(4, pairs[2], 0)
-        spent = rounded(5, pairs[2], 1)
-        quantize(pairs[2][:], [("w", 4, 1), ("w", 5, 1)])
+        add_on_gpsimd(0, 0, T // 2, "pair0")
+
+        round_on_scalar(unit_of(pairs[1], 0), w_raw[5, 1][:])
+        put_back(0, 2, w_raw[5, 1][:, 0, :])
+        round_on_scalar(unit_of(pairs[1], 1), w_raw[SHARED, 1][:])
+        quantize(pairs[1][:], [("w", 5, 1), ("w", SHARED, 1)])
         routed_products(2, 1)
-        add_on_gpsimd(0, 0, "pair2")
-        put_back(0, 2, spent[:, 0, :])
-        spent_tag = weights([SHARED], 1)
-        last = w_raw[SHARED, 1]
-        put_back(0, 3, last[:, 0, :])
+        rows = w_raw[SHARED, 1]
+        put_back(0, 3, rows[:, 0, :])
         shared_to_sbuf(0, 2 * BANK)
-        add_on_gpsimd(0, 1, spent_tag)
-        put_back(1, 2, last[:, 1, :])
+        add_on_gpsimd(0, T // 2, T, "pair1")
+        put_back(1, 2, rows[:, 1, :])
         shared_to_sbuf(1, 0, BANK, 2 * BANK)
-        add_on_gpsimd(1, 0)
-        add_on_gpsimd(1, 1)
-        put_back(2, 2, last[:, 2, :])
+        add_on_gpsimd(1, 0, T // 2)
+        add_on_gpsimd(1, T // 2, T)
+        put_back(2, 2, rows[:, 2, :])
         shared_to_sbuf(2, 0, BANK)
-        put_back(1, 3, last[:, 3, :])
+        put_back(1, 3, rows[:, 3, :])
         shared_to_sbuf(2, 2 * BANK)
-        put_back(2, 3, spent[:, 1, :])
-        add_on_gpsimd(2, 0)
-        add_on_gpsimd(2, 1)
-        add_on_vector(3)
+        put_back(2, 3, w_raw[5, 1][:, 1, :])
+        add_on_gpsimd(2, 0, T // 2)
+        add_on_gpsimd(2, T // 2, T)
+
+        add_on_vector(3, 0)
+        add_on_vector(3, BANK)
+        shared_to_sbuf(3, 2 * BANK)
+        add_on_gpsimd(3, 2 * BANK, T)

from contextlib import ExitStack

import concourse.mybir as mybir

K, T, E, C, N = 512, 1280, 6, 128, 512
S = E * C
FLOPS = 2 * N * K * (S + T)
BYTES = 4 * (N * T + (E + 1) * N * K + 128 * S + K * T) + 2 * 128 * (S // 16)

F32 = mybir.dt.float32
BF16 = mybir.dt.bfloat16
U32 = mybir.dt.uint32
U16 = mybir.dt.uint16
U8 = mybir.dt.uint8
FP8X4 = mybir.dt.float8_e4m3fn_x4
MULT = mybir.AluOpType.mult
ADD = mybir.AluOpType.add

P = 128
PACK = 4
COLS = 256
UNIT = COLS * PACK
BLOCKS = K // P
BANK = 512
SHARED = E
PER_COLUMN = 16


def tile_moe_bds_lin_none_kernel(tc, dyT, w, gate, offs, out):
    nc = tc.nc
    with ExitStack() as ctx:
        keep = ctx.enter_context(tc.tile_pool(name="keep", bufs=1))
        dx_psum = ctx.enter_context(tc.psum_pool(name="dx_psum", bufs=3))
        ds_psum = ctx.enter_context(tc.psum_pool(name="ds_psum", bufs=5))

        def sbuf(name, shape, dtype, tag=""):
            return keep.tile(shape, dtype, name=name, tag=tag, align_bytes=64)

        offsets = keep.tile([P, S // PER_COLUMN], U16, name="offsets")
        nc.sync.dma_start(offsets[:], offs)
        dy = sbuf("dy", [P, PACK, T], F32)
        dy_rows = dyT.rearrange("(p t) c -> p t c", t=PACK)
        for t in range(PACK):
            nc.sync.dma_start(dy[:, t, :], dy_rows[:, t, :])

        w_raw = {}

        def load_w(e, h):
            w_raw[e, h] = sbuf("w_raw%d_%d" % (e, h), [P, PACK, COLS], F32)
            rows = w[e].rearrange("(p t) k -> p t k", t=PACK)
            nc.sync.dma_start(w_raw[e, h][:], rows[:, :, h * COLS : (h + 1) * COLS])

        gates_first = sbuf("gates_first", [P, 2 * COLS], F32)
        nc.sync.dma_start(gates_first[:], gate[0:P, 0 : 2 * COLS])
        load_w(0, 0)
        load_w(1, 0)
        gates_last = sbuf("gates_last", [P, COLS], F32)
        nc.sync.dma_start(gates_last[:], gate[0:P, 2 * COLS : S])
        for e in range(2, E + 1):
            load_w(e, 0)
        for e in range(E + 1):
            load_w(e, 1)
        gates = [gates_first[:, 0:COLS], gates_first[:, COLS : 2 * COLS], gates_last[:]]

        routed = []
        for m in range(BLOCKS):
            window = sbuf("routed%d" % m, [P, T], F32)
            nc.gpsimd.memset(window[:].bitcast(U32), 0)
            routed.append(window)

        picked = sbuf("picked", [P, PACK, S], F32)
        for t in range(PACK):
            nc.vector.tensor_copy(picked[:, t, :], dy[:, t, :].indirect(offsets[:]))

        def dy_piece(c):
            return dy[:, :, c * COLS : (c + 1) * COLS]

        def unit_of(tile, i):
            return tile[:, i * UNIT : (i + 1) * UNIT]

        def round_on_scalar(dst, src):
            nc.scalar.copy(
                dst.rearrange("p (c i t) -> p c t i", i=4, t=PACK),
                src.rearrange("p t (c i) -> p c t i", i=4),
            )

        def round_on_gpsimd(dst, src):
            nc.gpsimd.tensor_scalar(
                dst.rearrange("p (c t) -> p c t", t=PACK), src.rearrange("p t c -> p c t"), 1.0, 0.0, MULT, ADD
            )

        def gate_and_round(dst, j):
            nc.vector.tensor_tensor(
                dst.rearrange("p (c i t) -> p c t i", i=2, t=PACK),
                picked[:, :, j * COLS : (j + 1) * COLS].rearrange("p t (c i) -> p c t i", i=2),
                gates[j].rearrange("p (c o i) -> p c o i", o=1, i=2).to_broadcast([P, COLS // 2, PACK, 2]),
                MULT,
            )

        mx = {}

        def quantize(src, keys, tag=""):
            width = COLS * len(keys)
            name = "_".join(str(part) for key in keys for part in key)
            words = sbuf("words_" + name, [P, width], U32, tag)
            scales = sbuf("scales_" + name, [P, width], U8)
            nc.vector.quantize_mx(out=words[:].bitcast(FP8X4), scales=scales[:], in_=src)
            for i, key in enumerate(keys):
                mx[key] = (words, scales, i * COLS)

        def product(acc, e, m, moving_key, lo, width):
            w_words, w_scales, w_at = mx["w", e, m // 2]
            words, scales, at = mx[moving_key]
            w_cols = slice(w_at + (m % 2) * P, w_at + (m % 2 + 1) * P)
            cols = slice(at + lo, at + lo + width)
            nc.tensor.matmul_mx(
                out=acc,
                lhsT=w_words[:, w_cols].bitcast(FP8X4),
                lhsT_scale=w_scales[:, w_cols],
                rhs=words[:, cols].bitcast(FP8X4),
                rhs_scale=scales[:, cols],
                start=True,
                stop=True,
            )

        dx_banks = {}

        def routed_products(j, h):
            bank = dx_psum.tile([P, BANK], F32, name="dx_bank")
            for i in range(2):
                for e in range(2):
                    at = i * COLS + e * C
                    product(bank[:, at : at + C], 2 * j + e, 2 * h + i, ("g", j), e * C, C)
            dx_banks[j, h] = bank

        def put_back(j, m, spent):
            nc.scalar.copy(spent, dx_banks[j, m // 2][:, (m % 2) * COLS : (m % 2 + 1) * COLS])
            entries = offsets[:, j * COLS // PER_COLUMN : (j + 1) * COLS // PER_COLUMN]
            nc.vector.tensor_copy(routed[m][:].indirect(entries), spent)

        def shared_product(m, lo):
            hi = min(lo + BANK, T)
            bank = ds_psum.tile([P, BANK], F32, name="ds_bank")
            for at in range(lo, hi, COLS):
                product(bank[:, at - lo : at - lo + COLS], SHARED, m, ("dy", at // COLS), 0, COLS)
            return bank[:, 0 : hi - lo]

        ds = [sbuf("ds%d" % m, [P, T], F32) for m in range(BLOCKS)]

        def shared_to_sbuf(m, *starts):
            for lo in starts:
                nc.scalar.copy(ds[m][:, lo : min(lo + BANK, T)], shared_product(m, lo))

        def add_on_gpsimd(m, lo, hi, tag=""):
            total = sbuf("total%d_%d" % (m, lo), [P, hi - lo], F32, tag)
            nc.gpsimd.tensor_tensor(total[:], ds[m][:, lo:hi], routed[m][:, lo:hi], ADD)
            nc.sync.dma_start(out[m * P : (m + 1) * P, lo:hi], total[:])

        def add_on_vector(m, lo):
            total = sbuf("total%d_%d" % (m, lo), [P, BANK], F32)
            nc.vector.tensor_tensor(total[:], shared_product(m, lo), routed[m][:, lo : lo + BANK], ADD)
            nc.sync.dma_start(out[m * P : (m + 1) * P, lo : lo + BANK], total[:])

        def lone_half(e, h):
            tag = "w_bf%d_%d" % (e, h)
            staged = sbuf(tag, [P, UNIT], BF16, tag)
            round_on_scalar(staged[:], w_raw[e, h][:])
            quantize(staged[:], [("w", e, h)])
            return tag

        early = sbuf("early", [P, 4 * UNIT], BF16)
        g_first = sbuf("g_first", [P, 2 * UNIT], BF16)
        for i in range(2):
            round_on_scalar(unit_of(early, i), dy_piece(i))
        round_on_gpsimd(unit_of(early, 2), dy_piece(2))
        for j in range(2):
            gate_and_round(unit_of(g_first, j), j)
        quantize(unit_of(g_first, 0), [("g", 0)])
        quantize(unit_of(g_first, 1), [("g", 1)], lone_half(0, 0))
        spent_unit = lone_half(1, 0)
        routed_products(0, 0)
        gate_and_round(unit_of(early, 3), 2)
        quantize(early[:], [("dy", 0), ("dy", 1), ("dy", 2), ("g", 2)], spent_unit)

        strip = sbuf("strip", [P, 8 * UNIT], BF16)

        def fill(first_unit, halves):
            for i, (e, h) in enumerate(halves):
                round_on_scalar(unit_of(strip, first_unit + i), w_raw[e, h][:])
            return [("w", e, h) for e, h in halves]

        quantize(strip[:, 0 : 2 * UNIT], fill(0, [(2, 0), (3, 0)]))
        routed_products(1, 0)
        round_on_gpsimd(unit_of(strip, 1), dy_piece(3))
        put_back(0, 0, w_raw[3, 0][:, 0, :])
        put_back(0, 1, w_raw[3, 0][:, 1, :])

        quantize(strip[:, UNIT : 5 * UNIT], [("dy", 3)] + fill(2, [(4, 0), (5, 0), (SHARED, 0)]))
        routed_products(2, 0)
        round_on_gpsimd(unit_of(strip, 4), dy_piece(4))
        put_back(1, 0, w_raw[SHARED, 0][:, 0, :])
        put_back(1, 1, w_raw[SHARED, 0][:, 1, :])

        quantize(strip[:, 4 * UNIT : 8 * UNIT], [("dy", 4)] + fill(5, [(0, 1), (1, 1), (2, 1)]))
        routed_products(0, 1)
        put_back(2, 0, w_raw[2, 1][:, 0, :])

        pairs = [sbuf("pair%d" % i, [P, 2 * UNIT], BF16, "pair%d" % i) for i in range(2)]
        for i in range(2):
            round_on_scalar(unit_of(pairs[0], i), w_raw[3 + i, 1][:])
        quantize(pairs[0][:], [("w", 3, 1), ("w", 4, 1)])
        routed_products(1, 1)
        put_back(2, 1, w_raw[4, 1][:, 0, :])
        shared_to_sbuf(0, 0, BANK)
        add_on_gpsimd(0, 0, T // 2, "pair0")

        round_on_scalar(unit_of(pairs[1], 0), w_raw[5, 1][:])
        put_back(0, 2, w_raw[5, 1][:, 0, :])
        round_on_scalar(unit_of(pairs[1], 1), w_raw[SHARED, 1][:])
        quantize(pairs[1][:], [("w", 5, 1), ("w", SHARED, 1)])
        routed_products(2, 1)
        rows = w_raw[SHARED, 1]
        put_back(0, 3, rows[:, 0, :])
        shared_to_sbuf(0, 2 * BANK)
        add_on_gpsimd(0, T // 2, T, "pair1")
        put_back(1, 2, rows[:, 1, :])
        shared_to_sbuf(1, 0, BANK, 2 * BANK)
        add_on_gpsimd(1, 0, T // 2)
        add_on_gpsimd(1, T // 2, T)
        put_back(2, 2, rows[:, 2, :])
        shared_to_sbuf(2, 0, BANK)
        put_back(1, 3, rows[:, 3, :])
        shared_to_sbuf(2, 2 * BANK)
        put_back(2, 3, w_raw[5, 1][:, 1, :])
        add_on_gpsimd(2, 0, T // 2)
        add_on_gpsimd(2, T // 2, T)

        add_on_vector(3, 0)
        add_on_vector(3, BANK)
        shared_to_sbuf(3, 2 * BANK)
        add_on_gpsimd(3, 2 * BANK, T)
